import numpy as np
import ml_dtypes


def mxq(x, axis, fmt="e4m3"):
    dtype, down = {"e4m3": (ml_dtypes.float8_e4m3fn, 7), "e5m2": (ml_dtypes.float8_e5m2, 14)}[fmt]
    v = np.moveaxis(np.asarray(x, np.float32).astype(ml_dtypes.bfloat16).astype(np.float64), axis, -1)
    blocks = v.reshape(v.shape[:-1] + (-1, 32))
    amax = np.abs(blocks).max(-1, keepdims=True)
    byte = np.maximum(np.where(amax > 0, np.frexp(amax)[1] - 1 + 127, 0) - down, 1)
    scale = np.exp2(byte - 127.0)
    codes = (blocks / scale).astype(np.float32).astype(dtype).astype(np.float64)
    return np.moveaxis((codes * scale).reshape(v.shape), -1, axis)


WIDE = False


def mx_kscale(k):
    if not WIDE:
        return np.ones(k)
    levels = np.array([10, -10, 5, -5, 0])
    if k % 512:
        return np.exp2(np.random.permutation(np.resize(levels, k // 32))).repeat(32)
    a = np.empty((k // 512, 16))
    for p in range(k // 512):
        a[p, :8] = np.random.permutation(np.resize(levels, 8))
        for g in range(8):
            far = levels[np.abs(levels - a[p, g]) >= 10]
            a[p, g + 8] = far[np.random.randint(len(far))]
    return np.exp2(a.ravel()).repeat(32)


def f64(x):
    return np.asarray(x).astype(np.float64)


def striped8(idx):
    return np.concatenate([v.reshape(-1, 16).T for v in idx]).astype(np.uint16)


def unstriped8(offs):
    return np.stack([offs[16 * g:16 * g + 16].T.reshape(-1) for g in range(8)]).astype(np.int64)


E2M1 = np.array([0.0, 0.5, 1.0, 1.5, 2.0, 3.0, 4.0, 6.0, -0.0, -0.5, -1.0, -1.5, -2.0, -3.0, -4.0, -6.0])


def pack_weight(w, fmt):
    k, n = w.shape
    w = f64(np.asarray(w, np.float32).astype(ml_dtypes.bfloat16)).reshape(k // 32, 32, n)
    amax = np.abs(w).max(1)
    if fmt == "e4m3":
        byte = np.frexp(amax)[1] - 1 + 127 - 7
    else:
        mant, ex = np.frexp(amax / 6.0)
        byte = np.where(mant > 0.5, ex, ex - 1) + 127
    byte = np.clip(np.where(amax > 0, byte, 1), 1, 254)
    scaled = (w * np.exp2(127.0 - byte)[:, None, :]).reshape(k, n).astype(np.float32)
    by_word = np.ascontiguousarray(scaled.reshape(k // 512, 128, 4, n).transpose(0, 1, 3, 2))
    if fmt == "e4m3":
        words = by_word.astype(ml_dtypes.float8_e4m3fn).view(np.uint8)
    else:
        c = by_word.astype(ml_dtypes.float4_e2m1fn).view(np.uint8) & 0xF
        words = (c[..., 0::2] | (c[..., 1::2] << 4)).reshape(k // 512, 128, 2 * n)
    return np.ascontiguousarray(words), np.ascontiguousarray(byte.astype(np.uint8).reshape(k // 512, 16, n))


def unpack_weight(words, scales, fmt):
    g, _, n = scales.shape
    words = np.ascontiguousarray(words).reshape(g, 128, n, -1)
    if fmt == "e4m3":
        vals = words.view(ml_dtypes.float8_e4m3fn).astype(np.float64)
    else:
        nib = np.empty((g, 128, n, 4), np.uint8)
        nib[..., 0::2] = words & 0xF
        nib[..., 1::2] = words >> 4
        vals = E2M1[nib]
    vals = vals * np.repeat(np.exp2(scales.astype(np.float64) - 127.0), 8, axis=1)[..., None]
    return vals.transpose(0, 1, 3, 2).reshape(g * 512, n)


def gelu(v):
    return 0.5 * v * (1.0 + np.tanh(np.sqrt(2.0 / np.pi) * (v + 0.044715 * v**3)))


K, M, T, S = 1536, 256, 2048, 1024


def setup_inputs():
    n = np.random.standard_normal
    s = mx_kscale(K)[:, None]
    p_w = pack_weight(n((K, M)) / np.sqrt(K) / s, "e4m3")
    return {
        "x": (n((K, S)) * s).astype(np.float32),
        "w_words": p_w[0],
        "w_scales": p_w[1],
        "b": (0.3 * n(256)).astype(np.float32),
        "wgo": np.repeat(np.random.uniform(0.5, 2.0, (8, S)), 16, axis=0).astype(np.float32),
        "offs": striped8(np.stack([np.random.permutation(T)[:S] for _ in range(8)])),
    }


def reference(x, w_words, w_scales, b, wgo, offs):
    x_ = mxq(f64(x), 0, "e4m3")
    w_ = unpack_weight(w_words, w_scales, "e4m3")
    y = w_.T @ x_
    place = unstriped8(offs)[np.arange(M) % 128 // 16]
    out = np.zeros((M, T))
    out[np.arange(M)[:, None], place] = f64(wgo)[np.arange(M) % 128] * (gelu(y + f64(b)[:, None]))
    return out

@@ -1,0 +1,113 @@
+from contextlib import ExitStack
+
+import concourse.mybir as mybir
+
+K, M, T, S = 1536, 256, 2048, 1024
+FLOPS = 2 * K * M * S
+
+F32 = mybir.dt.float32
+BF16 = mybir.dt.bfloat16
+U32 = mybir.dt.uint32
+I32 = mybir.dt.int32
+U16 = mybir.dt.uint16
+U8 = mybir.dt.uint8
+FP8X4 = mybir.dt.float8_e4m3fn_x4
+
+P = 128
+PASSES = K // 512
+HALF = S // 2
+ROW_TILES = M // P
+
+VECTOR_COLUMNS = {(0, 0): 256, (0, 1): 256, (0, 2): 256, (1, 0): 0, (1, 1): 128, (1, 2): 256}
+
+
+def tile_list_hscat_gelu_kernel(tc, x, w_words, w_scales, b, wgo, offs, out):
+    nc = tc.nc
+    gelu = mybir.ActivationFunctionType.Gelu_apprx_tanh
+    mult = mybir.AluOpType.mult
+
+    with ExitStack() as ctx:
+        keep = ctx.enter_context(tc.tile_pool(name="keep", bufs=1))
+        psum = ctx.enter_context(tc.psum_pool(name="psum", bufs=1))
+
+        offsets = keep.tile([P, S // 16], U16, name="offsets")
+        w_codes = keep.tile([P, PASSES, M], U32, name="w_codes", align_bytes=64)
+        w_planes = keep.tile([P, PASSES, M], U8, name="w_planes", align_bytes=64)
+        bias = keep.tile([P, ROW_TILES], F32, name="bias")
+        warm_in = keep.tile([P, 1], F32, name="warm_in")
+        warm_out = keep.tile([P, 1], F32, name="warm_out")
+        factor = [keep.tile([P, HALF], F32, name=f"factor{h}") for h in range(2)]
+        window = [keep.tile([P, T], F32, name=f"window{m}") for m in range(ROW_TILES)]
+        raw = {}
+        grouped = {}
+        x_codes = {}
+        x_plane = {}
+        for h in range(2):
+            for a in range(PASSES):
+                raw[h, a] = keep.tile([P, 4, HALF], F32, name=f"raw{h}{a}")
+                grouped[h, a] = keep.tile([P, HALF, 4], BF16, name=f"grouped{h}{a}", align_bytes=64)
+                x_codes[h, a] = keep.tile([P, HALF], U32, name=f"x_codes{h}{a}", align_bytes=64)
+                x_plane[h, a] = keep.tile([P, HALF], U8, name=f"x_plane{h}{a}", align_bytes=64)
+
+        nc.vector.memset(w_planes[:].rearrange("p a n -> p (a n)").bitcast(I32), 0)
+        nc.vector.memset(warm_in[:], 0.0)
+        nc.scalar.activation(warm_out[:], warm_in[:], gelu)
+        nc.scalar.dma_start(bias[:], b.rearrange("(m p) -> p m", p=P))
+        for q in range(4):
+            nc.scalar.dma_start(
+                w_planes[32 * q : 32 * q + 4, :, :].bitcast(I32),
+                w_scales[:, 4 * q : 4 * q + 4, :].rearrange("a r n -> r a n").bitcast(I32),
+            )
+        for m in range(ROW_TILES):
+            nc.vector.memset(window[m][:], 0.0)
+
+        def load(h, a):
+            rows = x[512 * a : 512 * (a + 1), HALF * h : HALF * (h + 1)]
+            nc.sync.dma_start(raw[h, a][:], rows.rearrange("(p j) w -> p j w", j=4))
+
+        load(0, 0)
+        load(0, 1)
+        nc.sync.dma_start(w_codes[:].bitcast(I32), w_words.rearrange("a p n i -> p a (n i)").bitcast(I32))
+        load(0, 2)
+        nc.sync.dma_start(offsets[:], offs)
+        nc.sync.dma_start(factor[0][:], wgo[:, 0:HALF])
+        load(1, 0)
+        load(1, 1)
+        load(1, 2)
+        nc.sync.dma_start(factor[1][:], wgo[:, HALF:S])
+
+        for h in range(2):
+            acc = [psum.tile([P, HALF], F32, name=f"acc{h}{m}") for m in range(ROW_TILES)]
+            for a in range(PASSES):
+                split = HALF - VECTOR_COLUMNS[h, a]
+                out_view = grouped[h, a]
+                in_view = raw[h, a][:].rearrange("p j w -> p w j")
+                nc.scalar.copy(out_view[:, 0:split, :], in_view[:, 0:split, :])
+                if split < HALF:
+                    nc.vector.tensor_copy(out_view[:, split:HALF, :], in_view[:, split:HALF, :])
+                nc.vector.quantize_mx(
+                    x_codes[h, a][:].bitcast(FP8X4),
+                    x_plane[h, a][:],
+                    out_view[:].rearrange("p w j -> p (w j)"),
+                )
+                for m in range(ROW_TILES):
+                    nc.tensor.matmul_mx(
+                        acc[m][:],
+                        lhsT=w_codes[:, a, P * m : P * (m + 1)].bitcast(FP8X4),
+                        lhsT_scale=w_planes[:, a, P * m : P * (m + 1)],
+                        rhs=x_codes[h, a][:].bitcast(FP8X4),
+                        rhs_scale=x_plane[h, a][:],
+                        start=(a == 0),
+                        stop=(a == PASSES - 1),
+                    )
+            for m in range(ROW_TILES):
+                active = keep.tile([P, HALF], F32, name=f"active{h}{m}")
+                nc.scalar.activation(active[:], acc[m][:], gelu, bias=bias[:, m : m + 1])
+                nc.vector.tensor_tensor(
+                    window[m][:].indirect(offsets[:, (HALF // 16) * h : (HALF // 16) * (h + 1)]),
+                    active[:],
+                    factor[h][:],
+                    mult,
+                )
+                if h == 1:
+                    nc.sync.dma_start(out[P * m : P * (m + 1), :], window[m][:])

@@ -18,7 +18,13 @@ PASSES = K // 512
 HALF = S // 2
 ROW_TILES = M // P
 
-VECTOR_COLUMNS = {(0, 0): 256, (0, 1): 256, (0, 2): 256, (1, 0): 0, (1, 1): 128, (1, 2): 256}
+
+GROUPS = {
+    (0, 0): [(0, 256), (256, 512)],
+    (0, 1): [(0, 512)],
+    (1, 0): [(0, 256), (256, 384), (384, 512)],
+    (1, 1): [(0, 512)],
+}
 
 
 def tile_list_hscat_gelu_kernel(tc, x, w_words, w_scales, b, wgo, offs, out):
@@ -31,7 +37,7 @@ def tile_list_hscat_gelu_kernel(tc, x, w_words, w_scales, b, wgo, offs, out):
         psum = ctx.enter_context(tc.psum_pool(name="psum", bufs=1))
 
         offsets = keep.tile([P, S // 16], U16, name="offsets")
-        w_codes = keep.tile([P, PASSES, M], U32, name="w_codes", align_bytes=64)
+        w_codes = [keep.tile([P, M], U32, name=f"w_codes{a}", align_bytes=64) for a in range(PASSES)]
         w_planes = keep.tile([P, PASSES, M], U8, name="w_planes", align_bytes=64)
         bias = keep.tile([P, ROW_TILES], F32, name="bias")
         warm_in = keep.tile([P, 1], F32, name="warm_in")
@@ -61,53 +67,95 @@ def tile_list_hscat_gelu_kernel(tc, x, w_words, w_scales, b, wgo, offs, out):
         for m in range(ROW_TILES):
             nc.vector.memset(window[m][:], 0.0)
 
-        def load(h, a):
-            rows = x[512 * a : 512 * (a + 1), HALF * h : HALF * (h + 1)]
-            nc.sync.dma_start(raw[h, a][:], rows.rearrange("(p j) w -> p j w", j=4))
+        def load(h, a, lo=0, hi=HALF):
+            rows = x[512 * a : 512 * (a + 1), HALF * h + lo : HALF * h + hi]
+            nc.sync.dma_start(raw[h, a][:, :, lo:hi], rows.rearrange("(p j) w -> p j w", j=4))
+
+        def load_w(a):
+            nc.sync.dma_start(w_codes[a][:].bitcast(I32), w_words[a].rearrange("p n i -> p (n i)").bitcast(I32))
 
         load(0, 0)
         load(0, 1)
-        nc.sync.dma_start(w_codes[:].bitcast(I32), w_words.rearrange("a p n i -> p a (n i)").bitcast(I32))
-        load(0, 2)
+        load_w(0)
+        load_w(1)
+        load(0, 2, 0, 256)
+        load(0, 2, 256, 512)
+        load_w(2)
+        load(1, 0, 0, 256)
         nc.sync.dma_start(offsets[:], offs)
         nc.sync.dma_start(factor[0][:], wgo[:, 0:HALF])
-        load(1, 0)
+        load(1, 0, 256, 512)
         load(1, 1)
-        load(1, 2)
+        load(1, 2, 0, 256)
+        load(1, 2, 256, 512)
         nc.sync.dma_start(factor[1][:], wgo[:, HALF:S])
 
-        for h in range(2):
-            acc = [psum.tile([P, HALF], F32, name=f"acc{h}{m}") for m in range(ROW_TILES)]
+        def interleave(engine_copy, h, a, lo, hi):
+            engine_copy(
+                grouped[h, a][:, lo:hi, :].rearrange("p (c i) t -> p c t i", i=4),
+                raw[h, a][:, :, lo:hi].rearrange("p t (c i) -> p c t i", i=4),
+            )
+
+        def quantize(h, a, lo, hi):
+            nc.vector.quantize_mx(
+                x_codes[h, a][:, lo:hi].bitcast(FP8X4),
+                x_plane[h, a][:, lo:hi],
+                grouped[h, a][:, lo:hi, :].rearrange("p w j -> p (w j)"),
+            )
+
+        active = {}
+
+        def product(h, m):
+            active[h, m] = keep.tile([P, HALF], F32, name=f"active{h}{m}")
+            acc = [psum.tile([P, hi - lo], F32, name=f"acc{h}{m}{lo}") for lo, hi in GROUPS[h, m]]
             for a in range(PASSES):
-                split = HALF - VECTOR_COLUMNS[h, a]
-                out_view = grouped[h, a]
-                in_view = raw[h, a][:].rearrange("p j w -> p w j")
-                nc.scalar.copy(out_view[:, 0:split, :], in_view[:, 0:split, :])
-                if split < HALF:
-                    nc.vector.tensor_copy(out_view[:, split:HALF, :], in_view[:, split:HALF, :])
-                nc.vector.quantize_mx(
-                    x_codes[h, a][:].bitcast(FP8X4),
-                    x_plane[h, a][:],
-                    out_view[:].rearrange("p w j -> p (w j)"),
-                )
-                for m in range(ROW_TILES):
+                for bank, (lo, hi) in zip(acc, GROUPS[h, m]):
                     nc.tensor.matmul_mx(
-                        acc[m][:],
-                        lhsT=w_codes[:, a, P * m : P * (m + 1)].bitcast(FP8X4),
+                        bank[:],
+                        lhsT=w_codes[a][:, P * m : P * (m + 1)].bitcast(FP8X4),
                         lhsT_scale=w_planes[:, a, P * m : P * (m + 1)],
-                        rhs=x_codes[h, a][:].bitcast(FP8X4),
-                        rhs_scale=x_plane[h, a][:],
+                        rhs=x_codes[h, a][:, lo:hi].bitcast(FP8X4),
+                        rhs_scale=x_plane[h, a][:, lo:hi],
                         start=(a == 0),
                         stop=(a == PASSES - 1),
                     )
-            for m in range(ROW_TILES):
-                active = keep.tile([P, HALF], F32, name=f"active{h}{m}")
-                nc.scalar.activation(active[:], acc[m][:], gelu, bias=bias[:, m : m + 1])
-                nc.vector.tensor_tensor(
-                    window[m][:].indirect(offsets[:, (HALF // 16) * h : (HALF // 16) * (h + 1)]),
-                    active[:],
-                    factor[h][:],
-                    mult,
-                )
-                if h == 1:
-                    nc.sync.dma_start(out[P * m : P * (m + 1), :], window[m][:])
+            for bank, (lo, hi) in zip(acc, GROUPS[h, m]):
+                nc.scalar.activation(active[h, m][:, lo:hi], bank[:], gelu, bias=bias[:, m : m + 1])
+
+        def place(h, m):
+            nc.vector.tensor_tensor(
+                window[m][:].indirect(offsets[:, (HALF // 16) * h : (HALF // 16) * (h + 1)]),
+                active[h, m][:],
+                factor[h][:],
+                mult,
+            )
+
+        def store(m):
+            nc.sync.dma_start(out[P * m : P * (m + 1), :], window[m][:])
+
+        by_s, by_v = nc.scalar.copy, nc.vector.tensor_copy
+        for a in range(2):
+            interleave(by_s, 0, a, 0, 256)
+            interleave(by_v, 0, a, 256, 512)
+            quantize(0, a, 0, 512)
+        for lo in (0, 256):
+            interleave(by_v, 0, 2, lo, lo + 160)
+            interleave(by_s, 0, 2, lo + 160, lo + 256)
+            quantize(0, 2, lo, lo + 256)
+        product(0, 0)
+        interleave(by_v, 1, 0, 0, 256)
+        quantize(1, 0, 0, 256)
+        place(0, 0)
+        product(0, 1)
+        interleave(by_s, 1, 0, 256, 512)
+        quantize(1, 0, 256, 512)
+        place(0, 1)
+        interleave(by_s, 1, 1, 0, 512)
+        quantize(1, 1, 0, 512)
+        for lo, hi in GROUPS[1, 0]:
+            interleave(by_s, 1, 2, lo, hi)
+            quantize(1, 2, lo, hi)
+        for m in range(ROW_TILES):
+            product(1, m)
+            place(1, m)
+            store(m)

@@ -20,10 +20,10 @@ ROW_TILES = M // P
 
 
 GROUPS = {
-    (0, 0): [(0, 256), (256, 512)],
+    (0, 0): [(0, 256), (256, 384), (384, 512)],
     (0, 1): [(0, 512)],
-    (1, 0): [(0, 256), (256, 384), (384, 512)],
-    (1, 1): [(0, 512)],
+    (1, 0): [(0, 256), (256, 512)],
+    (1, 1): [(0, 256), (256, 512)],
 }
 
 
@@ -37,7 +37,7 @@ def tile_list_hscat_gelu_kernel(tc, x, w_words, w_scales, b, wgo, offs, out):
         psum = ctx.enter_context(tc.psum_pool(name="psum", bufs=1))
 
         offsets = keep.tile([P, S // 16], U16, name="offsets")
-        w_codes = [keep.tile([P, M], U32, name=f"w_codes{a}", align_bytes=64) for a in range(PASSES)]
+        w_codes = [keep.tile([P, PASSES, P], U32, name=f"w_codes{m}", align_bytes=64) for m in range(ROW_TILES)]
         w_planes = keep.tile([P, PASSES, M], U8, name="w_planes", align_bytes=64)
         bias = keep.tile([P, ROW_TILES], F32, name="bias")
         warm_in = keep.tile([P, 1], F32, name="warm_in")
@@ -58,7 +58,6 @@ def tile_list_hscat_gelu_kernel(tc, x, w_words, w_scales, b, wgo, offs, out):
         nc.vector.memset(w_planes[:].rearrange("p a n -> p (a n)").bitcast(I32), 0)
         nc.vector.memset(warm_in[:], 0.0)
         nc.scalar.activation(warm_out[:], warm_in[:], gelu)
-        nc.scalar.dma_start(bias[:], b.rearrange("(m p) -> p m", p=P))
         for q in range(4):
             nc.scalar.dma_start(
                 w_planes[32 * q : 32 * q + 4, :, :].bitcast(I32),
@@ -71,21 +70,24 @@ def tile_list_hscat_gelu_kernel(tc, x, w_words, w_scales, b, wgo, offs, out):
             rows = x[512 * a : 512 * (a + 1), HALF * h + lo : HALF * h + hi]
             nc.sync.dma_start(raw[h, a][:, :, lo:hi], rows.rearrange("(p j) w -> p j w", j=4))
 
-        def load_w(a):
-            nc.sync.dma_start(w_codes[a][:].bitcast(I32), w_words[a].rearrange("p n i -> p (n i)").bitcast(I32))
+        def load_w(m, first, last):
+            words = w_words[first:last, :, P * m : P * (m + 1), :]
+            nc.sync.dma_start(w_codes[m][:, first:last, :].bitcast(I32), words.rearrange("a p n i -> p a (n i)").bitcast(I32))
 
         load(0, 0)
         load(0, 1)
-        load_w(0)
-        load_w(1)
+        load_w(0, 0, 1)
         load(0, 2, 0, 256)
         load(0, 2, 256, 512)
-        load_w(2)
+        load_w(0, 1, 3)
+        nc.sync.dma_start(bias[:], b.rearrange("(m p) -> p m", p=P))
         load(1, 0, 0, 256)
         nc.sync.dma_start(offsets[:], offs)
         nc.sync.dma_start(factor[0][:], wgo[:, 0:HALF])
+        load_w(1, 0, 3)
         load(1, 0, 256, 512)
-        load(1, 1)
+        load(1, 1, 0, 256)
+        load(1, 1, 256, 512)
         load(1, 2, 0, 256)
         load(1, 2, 256, 512)
         nc.sync.dma_start(factor[1][:], wgo[:, HALF:S])
@@ -112,7 +114,7 @@ def tile_list_hscat_gelu_kernel(tc, x, w_words, w_scales, b, wgo, offs, out):
                 for bank, (lo, hi) in zip(acc, GROUPS[h, m]):
                     nc.tensor.matmul_mx(
                         bank[:],
-                        lhsT=w_codes[a][:, P * m : P * (m + 1)].bitcast(FP8X4),
+                        lhsT=w_codes[m][:, a, :].bitcast(FP8X4),
                         lhsT_scale=w_planes[:, a, P * m : P * (m + 1)],
                         rhs=x_codes[h, a][:, lo:hi].bitcast(FP8X4),
                         rhs_scale=x_plane[h, a][:, lo:hi],
@@ -134,27 +136,36 @@ def tile_list_hscat_gelu_kernel(tc, x, w_words, w_scales, b, wgo, offs, out):
             nc.sync.dma_start(out[P * m : P * (m + 1), :], window[m][:])
 
         by_s, by_v = nc.scalar.copy, nc.vector.tensor_copy
-        for a in range(2):
-            interleave(by_s, 0, a, 0, 256)
-            interleave(by_v, 0, a, 256, 512)
-            quantize(0, a, 0, 512)
-        for lo in (0, 256):
-            interleave(by_v, 0, 2, lo, lo + 160)
-            interleave(by_s, 0, 2, lo + 160, lo + 256)
-            quantize(0, 2, lo, lo + 256)
+        interleave(by_s, 0, 0, 0, 256)
+        interleave(by_v, 0, 0, 256, 512)
+        quantize(0, 0, 0, 512)
+        interleave(by_v, 0, 1, 0, 256)
+        interleave(by_s, 0, 1, 256, 448)
+        interleave(by_v, 0, 1, 448, 512)
+        quantize(0, 1, 0, 256)
+        quantize(0, 1, 256, 512)
+        interleave(by_v, 0, 2, 0, 160)
+        interleave(by_s, 0, 2, 160, 256)
+        quantize(0, 2, 0, 256)
+        interleave(by_s, 0, 2, 256, 384)
+        interleave(by_v, 0, 2, 384, 512)
+        quantize(0, 2, 384, 512)
+        quantize(0, 2, 256, 384)
         product(0, 0)
         interleave(by_v, 1, 0, 0, 256)
-        quantize(1, 0, 0, 256)
         place(0, 0)
+        quantize(1, 0, 0, 256)
         product(0, 1)
         interleave(by_s, 1, 0, 256, 512)
-        quantize(1, 0, 256, 512)
         place(0, 1)
-        interleave(by_s, 1, 1, 0, 512)
-        quantize(1, 1, 0, 512)
-        for lo, hi in GROUPS[1, 0]:
-            interleave(by_s, 1, 2, lo, hi)
-            quantize(1, 2, lo, hi)
+        for a in (1, 2):
+            for lo in (0, 256):
+                interleave(by_s, 1, a, lo, lo + 256)
+        quantize(1, 1, 0, 256)
+        quantize(1, 0, 256, 512)
+        quantize(1, 2, 0, 256)
+        quantize(1, 1, 256, 512)
+        quantize(1, 2, 256, 512)
         for m in range(ROW_TILES):
             product(1, m)
             place(1, m)

@@ -81,10 +81,10 @@ def tile_list_hscat_gelu_kernel(tc, x, w_words, w_scales, b, wgo, offs, out):
         load(0, 2, 256, 512)
         load_w(0, 1, 3)
         nc.sync.dma_start(bias[:], b.rearrange("(m p) -> p m", p=P))
-        load(1, 0, 0, 256)
         nc.sync.dma_start(offsets[:], offs)
         nc.sync.dma_start(factor[0][:], wgo[:, 0:HALF])
         load_w(1, 0, 3)
+        load(1, 0, 0, 256)
         load(1, 0, 256, 512)
         load(1, 1, 0, 256)
         load(1, 1, 256, 512)
@@ -152,10 +152,10 @@ def tile_list_hscat_gelu_kernel(tc, x, w_words, w_scales, b, wgo, offs, out):
         quantize(0, 2, 384, 512)
         quantize(0, 2, 256, 384)
         product(0, 0)
-        interleave(by_v, 1, 0, 0, 256)
         place(0, 0)
-        quantize(1, 0, 0, 256)
         product(0, 1)
+        interleave(by_s, 1, 0, 0, 256)
+        quantize(1, 0, 0, 256)
         interleave(by_s, 1, 0, 256, 512)
         place(0, 1)
         for a in (1, 2):

from contextlib import ExitStack

import concourse.mybir as mybir

K, M, T, S = 1536, 256, 2048, 1024
FLOPS = 2 * K * M * S

F32 = mybir.dt.float32
BF16 = mybir.dt.bfloat16
U32 = mybir.dt.uint32
I32 = mybir.dt.int32
U16 = mybir.dt.uint16
U8 = mybir.dt.uint8
FP8X4 = mybir.dt.float8_e4m3fn_x4

P = 128
PASSES = K // 512
HALF = S // 2
ROW_TILES = M // P


GROUPS = {
    (0, 0): [(0, 256), (256, 384), (384, 512)],
    (0, 1): [(0, 512)],
    (1, 0): [(0, 256), (256, 512)],
    (1, 1): [(0, 256), (256, 512)],
}


def tile_list_hscat_gelu_kernel(tc, x, w_words, w_scales, b, wgo, offs, out):
    nc = tc.nc
    gelu = mybir.ActivationFunctionType.Gelu_apprx_tanh
    mult = mybir.AluOpType.mult

    with ExitStack() as ctx:
        keep = ctx.enter_context(tc.tile_pool(name="keep", bufs=1))
        psum = ctx.enter_context(tc.psum_pool(name="psum", bufs=1))

        offsets = keep.tile([P, S // 16], U16, name="offsets")
        w_codes = [keep.tile([P, PASSES, P], U32, name=f"w_codes{m}", align_bytes=64) for m in range(ROW_TILES)]
        w_planes = keep.tile([P, PASSES, M], U8, name="w_planes", align_bytes=64)
        bias = keep.tile([P, ROW_TILES], F32, name="bias")
        warm_in = keep.tile([P, 1], F32, name="warm_in")
        warm_out = keep.tile([P, 1], F32, name="warm_out")
        factor = [keep.tile([P, HALF], F32, name=f"factor{h}") for h in range(2)]
        window = [keep.tile([P, T], F32, name=f"window{m}") for m in range(ROW_TILES)]
        raw = {}
        grouped = {}
        x_codes = {}
        x_plane = {}
        for h in range(2):
            for a in range(PASSES):
                raw[h, a] = keep.tile([P, 4, HALF], F32, name=f"raw{h}{a}")
                grouped[h, a] = keep.tile([P, HALF, 4], BF16, name=f"grouped{h}{a}", align_bytes=64)
                x_codes[h, a] = keep.tile([P, HALF], U32, name=f"x_codes{h}{a}", align_bytes=64)
                x_plane[h, a] = keep.tile([P, HALF], U8, name=f"x_plane{h}{a}", align_bytes=64)

        nc.vector.memset(w_planes[:].rearrange("p a n -> p (a n)").bitcast(I32), 0)
        nc.vector.memset(warm_in[:], 0.0)
        nc.scalar.activation(warm_out[:], warm_in[:], gelu)
        for q in range(4):
            nc.scalar.dma_start(
                w_planes[32 * q : 32 * q + 4, :, :].bitcast(I32),
                w_scales[:, 4 * q : 4 * q + 4, :].rearrange("a r n -> r a n").bitcast(I32),
            )
        for m in range(ROW_TILES):
            nc.vector.memset(window[m][:], 0.0)

        def load(h, a, lo=0, hi=HALF):
            rows = x[512 * a : 512 * (a + 1), HALF * h + lo : HALF * h + hi]
            nc.sync.dma_start(raw[h, a][:, :, lo:hi], rows.rearrange("(p j) w -> p j w", j=4))

        def load_w(m, first, last):
            words = w_words[first:last, :, P * m : P * (m + 1), :]
            nc.sync.dma_start(w_codes[m][:, first:last, :].bitcast(I32), words.rearrange("a p n i -> p a (n i)").bitcast(I32))

        load(0, 0)
        load(0, 1)
        load_w(0, 0, 1)
        load(0, 2, 0, 256)
        load(0, 2, 256, 512)
        load_w(0, 1, 3)
        nc.sync.dma_start(bias[:], b.rearrange("(m p) -> p m", p=P))
        nc.sync.dma_start(offsets[:], offs)
        nc.sync.dma_start(factor[0][:], wgo[:, 0:HALF])
        load_w(1, 0, 3)
        load(1, 0, 0, 256)
        load(1, 0, 256, 512)
        load(1, 1, 0, 256)
        load(1, 1, 256, 512)
        load(1, 2, 0, 256)
        load(1, 2, 256, 512)
        nc.sync.dma_start(factor[1][:], wgo[:, HALF:S])

        def interleave(engine_copy, h, a, lo, hi):
            engine_copy(
                grouped[h, a][:, lo:hi, :].rearrange("p (c i) t -> p c t i", i=4),
                raw[h, a][:, :, lo:hi].rearrange("p t (c i) -> p c t i", i=4),
            )

        def quantize(h, a, lo, hi):
            nc.vector.quantize_mx(
                x_codes[h, a][:, lo:hi].bitcast(FP8X4),
                x_plane[h, a][:, lo:hi],
                grouped[h, a][:, lo:hi, :].rearrange("p w j -> p (w j)"),
            )

        active = {}

        def product(h, m):
            active[h, m] = keep.tile([P, HALF], F32, name=f"active{h}{m}")
            acc = [psum.tile([P, hi - lo], F32, name=f"acc{h}{m}{lo}") for lo, hi in GROUPS[h, m]]
            for a in range(PASSES):
                for bank, (lo, hi) in zip(acc, GROUPS[h, m]):
                    nc.tensor.matmul_mx(
                        bank[:],
                        lhsT=w_codes[m][:, a, :].bitcast(FP8X4),
                        lhsT_scale=w_planes[:, a, P * m : P * (m + 1)],
                        rhs=x_codes[h, a][:, lo:hi].bitcast(FP8X4),
                        rhs_scale=x_plane[h, a][:, lo:hi],
                        start=(a == 0),
                        stop=(a == PASSES - 1),
                    )
            for bank, (lo, hi) in zip(acc, GROUPS[h, m]):
                nc.scalar.activation(active[h, m][:, lo:hi], bank[:], gelu, bias=bias[:, m : m + 1])

        def place(h, m):
            nc.vector.tensor_tensor(
                window[m][:].indirect(offsets[:, (HALF // 16) * h : (HALF // 16) * (h + 1)]),
                active[h, m][:],
                factor[h][:],
                mult,
            )

        def store(m):
            nc.sync.dma_start(out[P * m : P * (m + 1), :], window[m][:])

        by_s, by_v = nc.scalar.copy, nc.vector.tensor_copy
        interleave(by_s, 0, 0, 0, 256)
        interleave(by_v, 0, 0, 256, 512)
        quantize(0, 0, 0, 512)
        interleave(by_v, 0, 1, 0, 256)
        interleave(by_s, 0, 1, 256, 448)
        interleave(by_v, 0, 1, 448, 512)
        quantize(0, 1, 0, 256)
        quantize(0, 1, 256, 512)
        interleave(by_v, 0, 2, 0, 160)
        interleave(by_s, 0, 2, 160, 256)
        quantize(0, 2, 0, 256)
        interleave(by_s, 0, 2, 256, 384)
        interleave(by_v, 0, 2, 384, 512)
        quantize(0, 2, 384, 512)
        quantize(0, 2, 256, 384)
        product(0, 0)
        place(0, 0)
        product(0, 1)
        interleave(by_s, 1, 0, 0, 256)
        quantize(1, 0, 0, 256)
        interleave(by_s, 1, 0, 256, 512)
        place(0, 1)
        for a in (1, 2):
            for lo in (0, 256):
                interleave(by_s, 1, a, lo, lo + 256)
        quantize(1, 1, 0, 256)
        quantize(1, 0, 256, 512)
        quantize(1, 2, 0, 256)
        quantize(1, 1, 256, 512)
        quantize(1, 2, 256, 512)
        for m in range(ROW_TILES):
            product(1, m)
            place(1, m)
            store(m)
